import numpy as np
import ml_dtypes


def mxq(x, axis, fmt="e4m3"):
    dtype, down = {"e4m3": (ml_dtypes.float8_e4m3fn, 7), "e5m2": (ml_dtypes.float8_e5m2, 14)}[fmt]
    v = np.moveaxis(np.asarray(x, np.float32).astype(ml_dtypes.bfloat16).astype(np.float64), axis, -1)
    blocks = v.reshape(v.shape[:-1] + (-1, 32))
    amax = np.abs(blocks).max(-1, keepdims=True)
    byte = np.maximum(np.where(amax > 0, np.frexp(amax)[1] - 1 + 127, 0) - down, 1)
    scale = np.exp2(byte - 127.0)
    codes = (blocks / scale).astype(np.float32).astype(dtype).astype(np.float64)
    return np.moveaxis((codes * scale).reshape(v.shape), -1, axis)


WIDE = False


def mx_kscale(k):
    if not WIDE:
        return np.ones(k)
    levels = np.array([10, -10, 5, -5, 0])
    if k % 512:
        return np.exp2(np.random.permutation(np.resize(levels, k // 32))).repeat(32)
    a = np.empty((k // 512, 16))
    for p in range(k // 512):
        a[p, :8] = np.random.permutation(np.resize(levels, 8))
        for g in range(8):
            far = levels[np.abs(levels - a[p, g]) >= 10]
            a[p, g + 8] = far[np.random.randint(len(far))]
    return np.exp2(a.ravel()).repeat(32)


def f64(x):
    return np.asarray(x).astype(np.float64)


def striped(idx):
    return np.tile(idx.reshape(-1, 16).T, (8, 1)).astype(np.uint16)


def unstriped(offs):
    return offs[:16].T.reshape(-1).astype(np.int64)


def striped8(idx):
    return np.concatenate([x.reshape(-1, 16).T for x in idx]).astype(np.uint16)


def runs(offs, k):
    lists = np.stack([offs[16 * r : 16 * r + 16].T.reshape(-1) for r in range(8)]).astype(np.int64)
    return lists[np.arange(k) % 512 // 64]


def pack_weight(w):
    k, n = w.shape
    w = f64(np.asarray(w, np.float32).astype(ml_dtypes.bfloat16)).reshape(k // 32, 32, n)
    amax = np.abs(w).max(1)
    byte = np.clip(np.where(amax > 0, np.frexp(amax)[1] - 1 + 127 - 7, 1), 1, 254)
    scaled = (w * np.exp2(127.0 - byte)[:, None, :]).reshape(k, n).astype(np.float32)
    words = np.ascontiguousarray(scaled.reshape(k // 512, 128, 4, n).transpose(0, 1, 3, 2)).astype(ml_dtypes.float8_e4m3fn).view(np.uint8)
    return words, np.ascontiguousarray(byte.astype(np.uint8).reshape(k // 512, 16, n))


def unpack_weight(words, scales):
    g, p, n, _ = words.shape
    vals = np.ascontiguousarray(words).view(ml_dtypes.float8_e4m3fn).astype(np.float64) * np.repeat(np.exp2(scales.astype(np.float64) - 127.0), 8, axis=1)[..., None]
    return vals.transpose(0, 1, 3, 2).reshape(g * 512, n)


def sigmoid(v):
    return 1.0 / (1.0 + np.exp(-np.maximum(v, -700.0)))


K, T, S, H, G = 512, 2048, 512, 512, 2048


def setup_inputs():
    n = np.random.standard_normal
    s = mx_kscale(K)[:, None]
    packed_xT = pack_weight(n((K, T)) * s)
    packed_dT = pack_weight(n((K, G)) / s)
    return {
        "x_words": packed_xT[0],
        "x_scales": packed_xT[1],
        "w1": (n((K, H)) / np.sqrt(K) / s).astype(np.float32),
        "gs": (np.random.uniform(0.5, 1.5, (K, 1)) * s).astype(np.float32),
        "d_words": packed_dT[0],
        "d_scales": packed_dT[1],
        "offs": striped(np.random.permutation(T)[:S]),
        "n1": striped8(np.stack([np.random.permutation(S) for _ in range(8)])),
        "n2": striped8(np.stack([np.random.permutation(S) for _ in range(8)])),
        "k1": striped8(np.random.randint(0, G, (8, H))),
        "n3": striped8(np.stack([np.random.permutation(S) for _ in range(8)])),
        "n4": striped8(np.stack([np.random.permutation(S) for _ in range(8)])),
    }


def reference(x_words, x_scales, w1, gs, d_words, d_scales, offs, n1, n2, k1, n3, n4):
    d_k1 = unpack_weight(d_words, d_scales)[np.arange(K)[:, None], runs(k1, K)]
    xq = unpack_weight(x_words, x_scales)[:, unstriped(offs)]
    y = mxq(f64(w1), 0, "e4m3").T @ xq
    z = f64(gs) * (y * (sigmoid(y[np.arange(H)[:, None], runs(n1, H)] - (y[np.arange(H)[:, None], runs(n2, H)]))))
    h = 0.0625 * ((d_k1.T @ mxq(z, 0, "e4m3")))
    return h + (sigmoid(h[np.arange(H)[:, None], runs(n3, H)])) * (h[np.arange(H)[:, None], runs(n4, H)] - h)

@@ -1,0 +1,221 @@
+from contextlib import ExitStack
+
+import concourse.mybir as mybir
+
+K, T, S, H, G = 512, 2048, 512, 512, 2048
+FLOPS = 2 * K * H * S + 2 * H * H * S
+
+F32 = mybir.dt.float32
+BF16 = mybir.dt.bfloat16
+I32 = mybir.dt.int32
+U32 = mybir.dt.uint32
+U16 = mybir.dt.uint16
+U8 = mybir.dt.uint8
+FP8X4 = mybir.dt.float8_e4m3fn_x4
+MULT = mybir.AluOpType.mult
+ADD = mybir.AluOpType.add
+SUB = mybir.AluOpType.subtract
+SIGMOID = mybir.ActivationFunctionType.Sigmoid
+COPY = mybir.ActivationFunctionType.Copy
+
+P = 128
+PACK = 4
+Z_CHUNKS = ((0, 256), (256, 384), (384, 512))
+OUT_CHUNKS = (
+    ((0, 128), (128, 256), (256, 512)),
+    ((0, 256), (256, 512)),
+    ((0, 256), (256, 512)),
+    ((0, 256), (256, 384), (384, 512)),
+)
+
+
+def tile_picked_densecmptrack_none_p_kernel(
+    tc, x_words, x_scales, w1, gs, d_words, d_scales, offs, n1, n2, k1, n3, n4, out
+):
+    nc = tc.nc
+    with ExitStack() as ctx:
+        keep = ctx.enter_context(tc.tile_pool(name="keep", bufs=1))
+        ring = ctx.enter_context(tc.tile_pool(name="ring", bufs=2))
+        psum = ctx.enter_context(tc.psum_pool(name="psum", bufs=1))
+
+        def load_list(name, src):
+            lst = keep.tile([P, S // 16], U16, name=name)
+            nc.sync.dma_start(lst[:], src)
+            return lst
+
+        def entries(lst, a, b):
+            return lst[:, a // 16 : b // 16]
+
+        x_sc = keep.tile([P, T], U8, name="x_sc")
+        d_sc = keep.tile([P, G], U8, name="d_sc")
+        nc.gpsimd.memset(x_sc[:].bitcast(I32), 0)
+        nc.gpsimd.memset(d_sc[:].bitcast(I32), 0)
+
+        offs_t = load_list("offs_t", offs)
+        w_view = w1.rearrange("(p j) c -> p j c", j=PACK)
+        w_raw = [keep.tile([P, PACK, H // 2], F32, name="w_raw%d" % a) for a in range(2)]
+        nc.sync.dma_start(w_raw[0][:], w_view[:, :, 0 : H // 2])
+        for q in range(4):
+            nc.sync.dma_start(x_sc[32 * q : 32 * q + 4, :].bitcast(I32), x_scales[0][4 * q : 4 * q + 4, :].bitcast(I32))
+        nc.sync.dma_start(w_raw[1][:], w_view[:, :, H // 2 : H])
+        x_w = keep.tile([P, T], U32, name="x_w")
+        nc.sync.dma_start(x_w[:].bitcast(I32), x_words[0].rearrange("p n t -> p (n t)").bitcast(I32))
+        k1_t = load_list("k1_t", k1)
+        d_rows = d_scales[0].rearrange("(g b) n -> b g n", b=2)
+        for b in range(2):
+            nc.sync.dma_start(d_sc[b:P:16, :].bitcast(I32), d_rows[b].bitcast(I32))
+        n2_t = load_list("n2_t", n2)
+        n1_t = load_list("n1_t", n1)
+        d_w = keep.tile([P, G], U32, name="d_w")
+        nc.sync.dma_start(d_w[:].bitcast(I32), d_words[0].rearrange("p n t -> p (n t)").bitcast(I32))
+        gs_t = keep.tile([P, PACK], F32, name="gs_t")
+        nc.sync.dma_start(gs_t[:], gs.rearrange("(p t) o -> p (t o)", t=PACK))
+        n3_t = load_list("n3_t", n3)
+        n4_t = load_list("n4_t", n4)
+
+        xg_sc = keep.tile([P, S], U8, name="xg_sc", align_bytes=64)
+        nc.vector.tensor_copy(xg_sc[:], x_sc[:].indirect(offs_t[:]))
+
+        w_bf = keep.tile([P, PACK * H], BF16, name="w_bf", align_bytes=64)
+        w_dst = w_bf[:].rearrange("p (t m j) -> p m j t", t=PACK, j=PACK)
+        nc.scalar.copy(w_dst[:, 0:64], w_raw[0][:].rearrange("p j (m t) -> p m j t", t=PACK))
+        nc.vector.tensor_copy(w_dst[:, 64:128], w_raw[1][:].rearrange("p j (m t) -> p m j t", t=PACK))
+        w_q = keep.tile([P, H], U32, name="w_q", align_bytes=64)
+        w_sc = keep.tile([P, H], U8, name="w_sc", align_bytes=64)
+        nc.vector.quantize_mx(out=w_q[:].bitcast(FP8X4), scales=w_sc[:], in_=w_bf[:])
+
+        xg_w = keep.tile([P, S], U32, name="xg_w", align_bytes=64)
+        y_ps = [psum.tile([P, S], F32, name="y_ps%d" % t) for t in range(PACK)]
+        y_sb = [keep.tile([P, S], F32, name="y_sb%d" % t) for t in range(PACK)]
+        for a, b in ((0, 256), (256, 512)):
+            nc.vector.tensor_copy(xg_w[:, a:b], x_w[:].indirect(entries(offs_t, a, b)))
+        for t in range(PACK):
+            m = slice(t * P, (t + 1) * P)
+            for a, b in ((0, 256), (256, 512)):
+                nc.tensor.matmul_mx(
+                    out=y_ps[t][:, a:b], lhsT=w_q[:, m].bitcast(FP8X4), lhsT_scale=w_sc[:, m],
+                    rhs=xg_w[:, a:b].bitcast(FP8X4), rhs_scale=xg_sc[:, a:b], start=True, stop=True,
+                )
+                nc.scalar.copy(y_sb[t][:, a:b], y_ps[t][:, a:b])
+
+        dg_sc = keep.tile([P, H], U8, name="dg_sc", align_bytes=64)
+        nc.vector.tensor_copy(dg_sc[:], d_sc[:].indirect(k1_t[:]))
+        dd_sc = keep.tile([P, H], U8, name="dd_sc", align_bytes=64)
+        nc.vector.tensor_copy(
+            dd_sc[:].rearrange("p (t m) -> p m t", t=PACK), dg_sc[:].rearrange("p (m t) -> p m t", t=PACK)
+        )
+        dm_sc = keep.tile([P, H], U8, name="dm_sc", align_bytes=64)
+        nc.vector.tensor_copy(dm_sc[:].bitcast(I32), dd_sc[:].bitcast(I32))
+        for b in range(2):
+            nc.sync.dma_start(dm_sc[2 + b : P : 32, :].bitcast(I32), dd_sc[16 + b : P : 32, :].bitcast(I32))
+
+        dg_w = keep.tile([P, H], U32, name="dg_w", align_bytes=64)
+        dd_w = keep.tile([P, H], U32, name="dd_w", align_bytes=64)
+
+        def dictionary_words():
+            nc.vector.tensor_copy(dg_w[:], d_w[:].indirect(k1_t[:]))
+            nc.vector.tensor_copy(
+                dd_w[:].bitcast(I32).rearrange("p (t m) -> p m t", t=PACK),
+                dg_w[:].bitcast(I32).rearrange("p (m t) -> p m t", t=PACK),
+            )
+
+        h_ps = [psum.tile([P, S], F32, name="h_ps%d" % t) for t in range(PACK)]
+        h_sb = [keep.tile([P, S], F32, name="h_sb%d" % t) for t in range(PACK)]
+        z_q = keep.tile([P, S], U32, name="z_q", align_bytes=64)
+        z_sc = keep.tile([P, S], U8, name="z_sc", align_bytes=64)
+        z_pl = [keep.tile([P, PACK, b - a], BF16, name="z_pl%d" % ci) for ci, (a, b) in enumerate(Z_CHUNKS)]
+        units = [(ci, t) for ci in range(len(Z_CHUNKS)) for t in range(PACK)]
+        second = {}
+        gates = {}
+
+        def fetch_second(u):
+            ci, t = units[u]
+            a, b = Z_CHUNKS[ci]
+            second[u] = ring.tile([P, b - a], F32, name="second")
+            nc.vector.tensor_copy(second[u][:], y_sb[t][:].indirect(entries(n2_t, a, b)))
+
+        def make_gate(u):
+            ci, t = units[u]
+            a, b = Z_CHUNKS[ci]
+            diff = ring.tile([P, b - a], F32, name="diff")
+            nc.vector.tensor_tensor(diff[:], y_sb[t][:].indirect(entries(n1_t, a, b)), second[u][:], SUB)
+            gates[u] = ring.tile([P, b - a], F32, name="gate")
+            nc.scalar.activation(gates[u][:], diff[:], SIGMOID)
+
+        def make_z(u):
+            ci, t = units[u]
+            a, b = Z_CHUNKS[ci]
+            nc.vector.scalar_tensor_tensor(
+                z_pl[ci][:, t, :], y_ps[t][:, a:b], gs_t[:, t : t + 1], gates[u][:], MULT, MULT
+            )
+
+        z_bf = {}
+
+        def interleave(ci):
+            a, b = Z_CHUNKS[ci]
+            z_bf[ci] = keep.tile([P, PACK * (b - a)], BF16, name="z_bf%d" % ci, align_bytes=64)
+            z_dst = z_bf[ci][:].rearrange("p (c i t) -> p c t i", i=8, t=PACK)
+            z_src = z_pl[ci][:].rearrange("p t (c i) -> p c t i", i=8)
+            if ci == len(Z_CHUNKS) - 1:
+                nc.vector.tensor_copy(z_dst, z_src)
+            else:
+                nc.scalar.copy(z_dst, z_src)
+
+        def second_product(ci):
+            a, b = Z_CHUNKS[ci]
+            nc.vector.quantize_mx(out=z_q[:, a:b].bitcast(FP8X4), scales=z_sc[:, a:b], in_=z_bf[ci][:])
+            for t in range(PACK):
+                m = slice(t * P, (t + 1) * P)
+                nc.tensor.matmul_mx(
+                    out=h_ps[t][:, a:b], lhsT=dd_w[:, m].bitcast(FP8X4), lhsT_scale=dm_sc[:, m],
+                    rhs=z_q[:, a:b].bitcast(FP8X4), rhs_scale=z_sc[:, a:b], start=True, stop=True,
+                )
+                nc.scalar.activation(h_sb[t][:, a:b], h_ps[t][:, a:b], COPY, scale=0.0625)
+
+        for step in range(len(units) + 2):
+            if step < len(units):
+                fetch_second(step)
+            if 0 <= step - 1 < len(units):
+                make_gate(step - 1)
+            if 0 <= step - 2 < len(units):
+                make_z(step - 2)
+                ci, t = units[step - 2]
+                if t == PACK - 1:
+                    interleave(ci)
+                    if ci == 0:
+                        dictionary_words()
+                if t == 1 and ci > 0:
+                    second_product(ci - 1)
+        second_product(len(Z_CHUNKS) - 1)
+
+        out_view = out.rearrange("(p t) j -> t p j", t=PACK)
+        pieces = [(t, a, b) for t in range(PACK) for a, b in OUT_CHUNKS[t]]
+        picked = {}
+        rest = {}
+        mix = {}
+
+        def fetch(u):
+            t, a, b = pieces[u]
+            mix[u] = ring.tile([P, b - a], F32, name="mix", bufs=3)
+            nc.scalar.activation(mix[u][:], h_sb[t][:].indirect(entries(n3_t, a, b)), SIGMOID)
+            picked[u] = ring.tile([P, b - a], F32, name="picked")
+            nc.vector.tensor_tensor(picked[u][:], h_sb[t][:].indirect(entries(n4_t, a, b)), mix[u][:], MULT)
+
+        def remainder(u):
+            t, a, b = pieces[u]
+            rest[u] = ring.tile([P, b - a], F32, name="rest")
+            nc.vector.scalar_tensor_tensor(rest[u][:], mix[u][:], 1.0, h_ps[t][:, a:b], SUB, MULT)
+
+        def finish(u):
+            t, a, b = pieces[u]
+            res = ring.tile([P, b - a], F32, name="res", bufs=4)
+            nc.vector.scalar_tensor_tensor(res[:], rest[u][:], -0.0625, picked[u][:], MULT, ADD)
+            nc.sync.dma_start(out_view[t][:, a:b], res[:])
+
+        for u in range(len(pieces) + 1):
+            if u < len(pieces):
+                fetch(u)
+            if u > 0:
+                finish(u - 1)
+            if u < len(pieces):
+                remainder(u)

@@ -20,11 +20,12 @@ COPY = mybir.ActivationFunctionType.Copy
 
 P = 128
 PACK = 4
+W_PARTS = ((0, 384), (384, 512))
 Z_CHUNKS = ((0, 256), (256, 384), (384, 512))
 OUT_CHUNKS = (
     ((0, 128), (128, 256), (256, 512)),
-    ((0, 256), (256, 512)),
-    ((0, 256), (256, 512)),
+    ((0, 512),),
+    ((0, 512),),
     ((0, 256), (256, 384), (384, 512)),
 )
 
@@ -49,21 +50,19 @@ def tile_picked_densecmptrack_none_p_kernel(
         x_sc = keep.tile([P, T], U8, name="x_sc")
         d_sc = keep.tile([P, G], U8, name="d_sc")
         nc.gpsimd.memset(x_sc[:].bitcast(I32), 0)
-        nc.gpsimd.memset(d_sc[:].bitcast(I32), 0)
+        nc.vector.memset(d_sc[:].bitcast(I32), 0)
 
         offs_t = load_list("offs_t", offs)
         w_view = w1.rearrange("(p j) c -> p j c", j=PACK)
-        w_raw = [keep.tile([P, PACK, H // 2], F32, name="w_raw%d" % a) for a in range(2)]
-        nc.sync.dma_start(w_raw[0][:], w_view[:, :, 0 : H // 2])
-        for q in range(4):
-            nc.sync.dma_start(x_sc[32 * q : 32 * q + 4, :].bitcast(I32), x_scales[0][4 * q : 4 * q + 4, :].bitcast(I32))
-        nc.sync.dma_start(w_raw[1][:], w_view[:, :, H // 2 : H])
-        x_w = keep.tile([P, T], U32, name="x_w")
-        nc.sync.dma_start(x_w[:].bitcast(I32), x_words[0].rearrange("p n t -> p (n t)").bitcast(I32))
+        w_raw = [keep.tile([P, PACK, b - a], F32, name="w_raw%d" % a) for a, b in W_PARTS]
+        nc.sync.dma_start(w_raw[0][:], w_view[:, :, W_PARTS[0][0] : W_PARTS[0][1]])
         k1_t = load_list("k1_t", k1)
-        d_rows = d_scales[0].rearrange("(g b) n -> b g n", b=2)
-        for b in range(2):
-            nc.sync.dma_start(d_sc[b:P:16, :].bitcast(I32), d_rows[b].bitcast(I32))
+        for q in range(4):
+            nc.scalar.dma_start(x_sc[32 * q : 32 * q + 4, :].bitcast(I32), x_scales[0][4 * q : 4 * q + 4, :].bitcast(I32))
+        nc.scalar.dma_start(d_sc[0:P:8, :].bitcast(I32), d_scales[0].bitcast(I32))
+        nc.sync.dma_start(w_raw[1][:], w_view[:, :, W_PARTS[1][0] : W_PARTS[1][1]])
+        x_w = keep.tile([P, T], U32, name="x_w", tag="x_w", align_bytes=64)
+        nc.sync.dma_start(x_w[:].bitcast(I32), x_words[0].rearrange("p n t -> p (n t)").bitcast(I32))
         n2_t = load_list("n2_t", n2)
         n1_t = load_list("n1_t", n1)
         d_w = keep.tile([P, G], U32, name="d_w")
@@ -78,15 +77,19 @@ def tile_picked_densecmptrack_none_p_kernel(
 
         w_bf = keep.tile([P, PACK * H], BF16, name="w_bf", align_bytes=64)
         w_dst = w_bf[:].rearrange("p (t m j) -> p m j t", t=PACK, j=PACK)
-        nc.scalar.copy(w_dst[:, 0:64], w_raw[0][:].rearrange("p j (m t) -> p m j t", t=PACK))
-        nc.vector.tensor_copy(w_dst[:, 64:128], w_raw[1][:].rearrange("p j (m t) -> p m j t", t=PACK))
+        nc.scalar.copy(w_dst[:, 0:96], w_raw[0][:].rearrange("p j (m t) -> p m j t", t=PACK))
+        nc.scalar.copy(w_dst[:, 96:128], w_raw[1][:].rearrange("p j (m t) -> p m j t", t=PACK))
         w_q = keep.tile([P, H], U32, name="w_q", align_bytes=64)
         w_sc = keep.tile([P, H], U8, name="w_sc", align_bytes=64)
         nc.vector.quantize_mx(out=w_q[:].bitcast(FP8X4), scales=w_sc[:], in_=w_bf[:])
 
+        dg_sc = keep.tile([P, H], U8, name="dg_sc", align_bytes=64)
+        nc.vector.tensor_copy(dg_sc[:], d_sc[:].indirect(k1_t[:]))
         xg_w = keep.tile([P, S], U32, name="xg_w", align_bytes=64)
         y_ps = [psum.tile([P, S], F32, name="y_ps%d" % t) for t in range(PACK)]
-        y_sb = [keep.tile([P, S], F32, name="y_sb%d" % t) for t in range(PACK)]
+        y_sb = [keep.tile([P, 2 * S if t < 2 else S], F32, name="y_sb%d" % t) for t in range(PACK)]
+        for t in range(2):
+            nc.vector.memset(y_sb[t][:, S : 2 * S], 0.0)
         for a, b in ((0, 256), (256, 512)):
             nc.vector.tensor_copy(xg_w[:, a:b], x_w[:].indirect(entries(offs_t, a, b)))
         for t in range(PACK):
@@ -98,16 +101,14 @@ def tile_picked_densecmptrack_none_p_kernel(
                 )
                 nc.scalar.copy(y_sb[t][:, a:b], y_ps[t][:, a:b])
 
-        dg_sc = keep.tile([P, H], U8, name="dg_sc", align_bytes=64)
-        nc.vector.tensor_copy(dg_sc[:], d_sc[:].indirect(k1_t[:]))
-        dd_sc = keep.tile([P, H], U8, name="dd_sc", align_bytes=64)
+        dd_sc = keep.tile([P, H], U8, name="dd_sc", tag="x_w", align_bytes=64)
         nc.vector.tensor_copy(
             dd_sc[:].rearrange("p (t m) -> p m t", t=PACK), dg_sc[:].rearrange("p (m t) -> p m t", t=PACK)
         )
         dm_sc = keep.tile([P, H], U8, name="dm_sc", align_bytes=64)
         nc.vector.tensor_copy(dm_sc[:].bitcast(I32), dd_sc[:].bitcast(I32))
-        for b in range(2):
-            nc.sync.dma_start(dm_sc[2 + b : P : 32, :].bitcast(I32), dd_sc[16 + b : P : 32, :].bitcast(I32))
+        for r in range(1, 4):
+            nc.sync.dma_start(dm_sc[r:P:32, :].bitcast(I32), dd_sc[8 * r : P : 32, :].bitcast(I32))
 
         dg_w = keep.tile([P, H], U32, name="dg_w", align_bytes=64)
         dd_w = keep.tile([P, H], U32, name="dd_w", align_bytes=64)
@@ -120,102 +121,132 @@ def tile_picked_densecmptrack_none_p_kernel(
             )
 
         h_ps = [psum.tile([P, S], F32, name="h_ps%d" % t) for t in range(PACK)]
-        h_sb = [keep.tile([P, S], F32, name="h_sb%d" % t) for t in range(PACK)]
+        h_sb = [keep.tile([P, 2 * S], F32, name="h_sb%d" % t) for t in range(PACK)]
+        for t in range(PACK):
+            (nc.gpsimd if t < 2 else nc.vector).memset(h_sb[t][:, S : 2 * S], 0.0)
         z_q = keep.tile([P, S], U32, name="z_q", align_bytes=64)
         z_sc = keep.tile([P, S], U8, name="z_sc", align_bytes=64)
-        z_pl = [keep.tile([P, PACK, b - a], BF16, name="z_pl%d" % ci) for ci, (a, b) in enumerate(Z_CHUNKS)]
-        units = [(ci, t) for ci in range(len(Z_CHUNKS)) for t in range(PACK)]
+        units = [(0, 0, 512), (1, 0, 512), (2, 0, 256), (3, 0, 256), (2, 256, 512), (3, 256, 384), (3, 384, 512)]
         second = {}
         gates = {}
 
         def fetch_second(u):
-            ci, t = units[u]
-            a, b = Z_CHUNKS[ci]
+            t, a, b = units[u]
             second[u] = ring.tile([P, b - a], F32, name="second")
             nc.vector.tensor_copy(second[u][:], y_sb[t][:].indirect(entries(n2_t, a, b)))
 
         def make_gate(u):
-            ci, t = units[u]
-            a, b = Z_CHUNKS[ci]
+            t, a, b = units[u]
             diff = ring.tile([P, b - a], F32, name="diff")
             nc.vector.tensor_tensor(diff[:], y_sb[t][:].indirect(entries(n1_t, a, b)), second[u][:], SUB)
-            gates[u] = ring.tile([P, b - a], F32, name="gate")
+            gates[u] = ring.tile([P, b - a], F32, name="gate", bufs=3)
             nc.scalar.activation(gates[u][:], diff[:], SIGMOID)
 
         def make_z(u):
-            ci, t = units[u]
-            a, b = Z_CHUNKS[ci]
+            t, a, b = units[u]
             nc.vector.scalar_tensor_tensor(
-                z_pl[ci][:, t, :], y_ps[t][:, a:b], gs_t[:, t : t + 1], gates[u][:], MULT, MULT
+                z_all[:, t, a:b], y_ps[t][:, a:b], gs_t[:, t : t + 1], gates[u][:], MULT, MULT
             )
 
+        z_all = keep.tile([P, PACK, S], BF16, name="z_all")
         z_bf = {}
 
         def interleave(ci):
             a, b = Z_CHUNKS[ci]
             z_bf[ci] = keep.tile([P, PACK * (b - a)], BF16, name="z_bf%d" % ci, align_bytes=64)
             z_dst = z_bf[ci][:].rearrange("p (c i t) -> p c t i", i=8, t=PACK)
-            z_src = z_pl[ci][:].rearrange("p t (c i) -> p c t i", i=8)
+            z_src = z_all[:, :, a:b].rearrange("p t (c i) -> p c t i", i=8)
             if ci == len(Z_CHUNKS) - 1:
                 nc.vector.tensor_copy(z_dst, z_src)
             else:
                 nc.scalar.copy(z_dst, z_src)
 
-        def second_product(ci):
+        def quantize_z(ci):
             a, b = Z_CHUNKS[ci]
             nc.vector.quantize_mx(out=z_q[:, a:b].bitcast(FP8X4), scales=z_sc[:, a:b], in_=z_bf[ci][:])
-            for t in range(PACK):
-                m = slice(t * P, (t + 1) * P)
-                nc.tensor.matmul_mx(
-                    out=h_ps[t][:, a:b], lhsT=dd_w[:, m].bitcast(FP8X4), lhsT_scale=dm_sc[:, m],
-                    rhs=z_q[:, a:b].bitcast(FP8X4), rhs_scale=z_sc[:, a:b], start=True, stop=True,
-                )
-                nc.scalar.activation(h_sb[t][:, a:b], h_ps[t][:, a:b], COPY, scale=0.0625)
 
-        for step in range(len(units) + 2):
-            if step < len(units):
-                fetch_second(step)
-            if 0 <= step - 1 < len(units):
-                make_gate(step - 1)
-            if 0 <= step - 2 < len(units):
-                make_z(step - 2)
-                ci, t = units[step - 2]
-                if t == PACK - 1:
-                    interleave(ci)
-                    if ci == 0:
-                        dictionary_words()
-                if t == 1 and ci > 0:
-                    second_product(ci - 1)
-        second_product(len(Z_CHUNKS) - 1)
+        def second_product(t, a, b):
+            m = slice(t * P, (t + 1) * P)
+            nc.tensor.matmul_mx(
+                out=h_ps[t][:, a:b], lhsT=dd_w[:, m].bitcast(FP8X4), lhsT_scale=dm_sc[:, m],
+                rhs=z_q[:, a:b].bitcast(FP8X4), rhs_scale=z_sc[:, a:b], start=True, stop=True,
+            )
+
+        def leave_bank(t, a, b):
+            nc.scalar.activation(h_sb[t][:, a:b], h_ps[t][:, a:b], COPY, scale=0.0625)
+
+        fetch_second(0)
+        fetch_second(1)
+        make_gate(0)
+        fetch_second(2)
+        make_gate(1)
+        make_z(0)
+        fetch_second(3)
+        make_gate(2)
+        make_z(1)
+        fetch_second(4)
+        make_gate(3)
+        make_z(2)
+        dictionary_words()
+        make_z(3)
+        interleave(0)
+        fetch_second(5)
+        make_gate(4)
+        fetch_second(6)
+        make_gate(5)
+        quantize_z(0)
+        for t in range(PACK):
+            second_product(t, 0, 256)
+        leave_bank(0, 0, 256)
+        make_gate(6)
+        make_z(4)
+        make_z(5)
+        interleave(1)
+        make_z(6)
+        interleave(2)
+        quantize_z(1)
+        quantize_z(2)
+        second_product(0, 256, 384)
+        second_product(0, 384, 512)
+        leave_bank(0, 256, 512)
+        for t in range(1, PACK):
+            second_product(t, 256, 512)
 
         out_view = out.rearrange("(p t) j -> t p j", t=PACK)
-        pieces = [(t, a, b) for t in range(PACK) for a, b in OUT_CHUNKS[t]]
         picked = {}
         rest = {}
         mix = {}
 
-        def fetch(u):
-            t, a, b = pieces[u]
-            mix[u] = ring.tile([P, b - a], F32, name="mix", bufs=3)
-            nc.scalar.activation(mix[u][:], h_sb[t][:].indirect(entries(n3_t, a, b)), SIGMOID)
-            picked[u] = ring.tile([P, b - a], F32, name="picked")
-            nc.vector.tensor_tensor(picked[u][:], h_sb[t][:].indirect(entries(n4_t, a, b)), mix[u][:], MULT)
+        def fetch(t):
+            mix[t] = ring.tile([P, S], F32, name="mix", bufs=3)
+            nc.scalar.activation(mix[t][:], h_sb[t][:].indirect(n3_t[:]), SIGMOID)
+            picked[t] = ring.tile([P, S], F32, name="picked")
+            if t == 0:
+                plain = keep.tile([P, S], F32, name="plain")
+                nc.vector.tensor_copy(plain[:], h_sb[t][:].indirect(n4_t[:]))
+                remainder(t, 0, S)
+                nc.vector.tensor_tensor(picked[t][:], plain[:], mix[t][:], MULT)
+            else:
+                nc.vector.tensor_tensor(picked[t][:], h_sb[t][:].indirect(n4_t[:]), mix[t][:], MULT)
 
-        def remainder(u):
-            t, a, b = pieces[u]
-            rest[u] = ring.tile([P, b - a], F32, name="rest")
-            nc.vector.scalar_tensor_tensor(rest[u][:], mix[u][:], 1.0, h_ps[t][:, a:b], SUB, MULT)
+        def remainder(t, a, b):
+            rest[t, a] = ring.tile([P, b - a], F32, name="rest", bufs=3)
+            nc.vector.scalar_tensor_tensor(rest[t, a][:], mix[t][:, a:b], 1.0, h_ps[t][:, a:b], SUB, MULT)
 
-        def finish(u):
-            t, a, b = pieces[u]
+        def finish(t, a, b):
             res = ring.tile([P, b - a], F32, name="res", bufs=4)
-            nc.vector.scalar_tensor_tensor(res[:], rest[u][:], -0.0625, picked[u][:], MULT, ADD)
+            nc.vector.scalar_tensor_tensor(res[:], rest[t, a][:], -0.0625, picked[t][:, a:b], MULT, ADD)
             nc.sync.dma_start(out_view[t][:, a:b], res[:])
 
-        for u in range(len(pieces) + 1):
-            if u < len(pieces):
-                fetch(u)
-            if u > 0:
-                finish(u - 1)
-            if u < len(pieces):
-                remainder(u)
+        fetch(0)
+        for t in range(1, PACK):
+            leave_bank(t, 0, 256)
+            leave_bank(t, 256, 512)
+            fetch(t)
+            finish(t - 1, 0, S)
+            if t < PACK - 1:
+                remainder(t, 0, S)
+        remainder(3, 0, 256)
+        remainder(3, 256, 512)
+        finish(3, 0, 256)
+        finish(3, 256, 512)

@@ -20,7 +20,7 @@ COPY = mybir.ActivationFunctionType.Copy
 
 P = 128
 PACK = 4
-W_PARTS = ((0, 384), (384, 512))
+W_PARTS = ((0, 256), (256, 512))
 Z_CHUNKS = ((0, 256), (256, 384), (384, 512))
 OUT_CHUNKS = (
     ((0, 128), (128, 256), (256, 512)),
@@ -58,8 +58,8 @@ def tile_picked_densecmptrack_none_p_kernel(
         nc.sync.dma_start(w_raw[0][:], w_view[:, :, W_PARTS[0][0] : W_PARTS[0][1]])
         k1_t = load_list("k1_t", k1)
         for q in range(4):
-            nc.scalar.dma_start(x_sc[32 * q : 32 * q + 4, :].bitcast(I32), x_scales[0][4 * q : 4 * q + 4, :].bitcast(I32))
-        nc.scalar.dma_start(d_sc[0:P:8, :].bitcast(I32), d_scales[0].bitcast(I32))
+            nc.sync.dma_start(x_sc[32 * q : 32 * q + 4, :].bitcast(I32), x_scales[0][4 * q : 4 * q + 4, :].bitcast(I32))
+        nc.sync.dma_start(d_sc[0:P:8, :].bitcast(I32), d_scales[0].bitcast(I32))
         nc.sync.dma_start(w_raw[1][:], w_view[:, :, W_PARTS[1][0] : W_PARTS[1][1]])
         x_w = keep.tile([P, T], U32, name="x_w", tag="x_w", align_bytes=64)
         nc.sync.dma_start(x_w[:].bitcast(I32), x_words[0].rearrange("p n t -> p (n t)").bitcast(I32))
@@ -77,8 +77,8 @@ def tile_picked_densecmptrack_none_p_kernel(
 
         w_bf = keep.tile([P, PACK * H], BF16, name="w_bf", align_bytes=64)
         w_dst = w_bf[:].rearrange("p (t m j) -> p m j t", t=PACK, j=PACK)
-        nc.scalar.copy(w_dst[:, 0:96], w_raw[0][:].rearrange("p j (m t) -> p m j t", t=PACK))
-        nc.scalar.copy(w_dst[:, 96:128], w_raw[1][:].rearrange("p j (m t) -> p m j t", t=PACK))
+        nc.scalar.copy(w_dst[:, 0:64], w_raw[0][:].rearrange("p j (m t) -> p m j t", t=PACK))
+        nc.scalar.copy(w_dst[:, 64:128], w_raw[1][:].rearrange("p j (m t) -> p m j t", t=PACK))
         w_q = keep.tile([P, H], U32, name="w_q", align_bytes=64)
         w_sc = keep.tile([P, H], U8, name="w_sc", align_bytes=64)
         nc.vector.quantize_mx(out=w_q[:].bitcast(FP8X4), scales=w_sc[:], in_=w_bf[:])
@@ -213,40 +213,60 @@ def tile_picked_densecmptrack_none_p_kernel(
             second_product(t, 256, 512)
 
         out_view = out.rearrange("(p t) j -> t p j", t=PACK)
-        picked = {}
-        rest = {}
-        mix = {}
+        mix = [keep.tile([P, S], F32, name="mix%d" % t) for t in range(PACK)]
+        picked = [keep.tile([P, S], F32, name="picked%d" % t) for t in range(PACK)]
+        step = [keep.tile([P, S], F32, name="step%d" % t) for t in range(PACK)]
+        part = [keep.tile([P, S], F32, name="part%d" % t) for t in range(PACK)]
 
-        def fetch(t):
-            mix[t] = ring.tile([P, S], F32, name="mix", bufs=3)
+        def weigh(t):
             nc.scalar.activation(mix[t][:], h_sb[t][:].indirect(n3_t[:]), SIGMOID)
-            picked[t] = ring.tile([P, S], F32, name="picked")
-            if t == 0:
-                plain = keep.tile([P, S], F32, name="plain")
-                nc.vector.tensor_copy(plain[:], h_sb[t][:].indirect(n4_t[:]))
-                remainder(t, 0, S)
-                nc.vector.tensor_tensor(picked[t][:], plain[:], mix[t][:], MULT)
-            else:
-                nc.vector.tensor_tensor(picked[t][:], h_sb[t][:].indirect(n4_t[:]), mix[t][:], MULT)
 
-        def remainder(t, a, b):
-            rest[t, a] = ring.tile([P, b - a], F32, name="rest", bufs=3)
-            nc.vector.scalar_tensor_tensor(rest[t, a][:], mix[t][:, a:b], 1.0, h_ps[t][:, a:b], SUB, MULT)
+        def pick(t, a, b):
+            nc.vector.tensor_copy(picked[t][:, a:b], h_sb[t][:].indirect(entries(n4_t, a, b)))
+
+        def differ(t, a, b):
+            nc.vector.scalar_tensor_tensor(step[t][:, a:b], h_ps[t][:, a:b], -0.0625, picked[t][:, a:b], MULT, ADD)
+
+        def scale(t, a, b):
+            nc.gpsimd.tensor_tensor(part[t][:, a:b], step[t][:, a:b], mix[t][:, a:b], MULT)
 
         def finish(t, a, b):
-            res = ring.tile([P, b - a], F32, name="res", bufs=4)
-            nc.vector.scalar_tensor_tensor(res[:], rest[t, a][:], -0.0625, picked[t][:, a:b], MULT, ADD)
+            res = ring.tile([P, b - a], F32, name="res", bufs=5)
+            if t == 0:
+                nc.gpsimd.tensor_tensor(res[:], part[t][:, a:b], h_sb[t][:, a:b], ADD)
+            else:
+                nc.vector.scalar_tensor_tensor(res[:], h_ps[t][:, a:b], 0.0625, part[t][:, a:b], MULT, ADD)
             nc.sync.dma_start(out_view[t][:, a:b], res[:])
 
-        fetch(0)
-        for t in range(1, PACK):
-            leave_bank(t, 0, 256)
-            leave_bank(t, 256, 512)
-            fetch(t)
-            finish(t - 1, 0, S)
-            if t < PACK - 1:
-                remainder(t, 0, S)
-        remainder(3, 0, 256)
-        remainder(3, 256, 512)
+        leave_bank(1, 0, 256)
+        leave_bank(1, 256, 512)
+        weigh(0)
+        leave_bank(2, 0, 256)
+        leave_bank(2, 256, 512)
+        weigh(1)
+        leave_bank(3, 0, 256)
+        leave_bank(3, 256, 512)
+        weigh(2)
+        weigh(3)
+        pick(0, 0, 256)
+        pick(0, 256, 512)
+        differ(0, 0, 256)
+        scale(0, 0, 256)
+        differ(0, 256, 512)
+        scale(0, 256, 512)
+        finish(0, 0, S)
+        pick(1, 0, S)
+        pick(2, 0, S)
+        differ(1, 0, S)
+        scale(1, 0, S)
+        differ(2, 0, S)
+        scale(2, 0, S)
+        pick(3, 0, S)
+        finish(1, 0, S)
+        differ(3, 0, 256)
+        scale(3, 0, 256)
+        differ(3, 256, 512)
+        scale(3, 256, 512)
+        finish(2, 0, S)
         finish(3, 0, 256)
         finish(3, 256, 512)

@@ -52,11 +52,14 @@ def tile_picked_densecmptrack_none_p_kernel(
         nc.gpsimd.memset(x_sc[:].bitcast(I32), 0)
         nc.vector.memset(d_sc[:].bitcast(I32), 0)
 
+        warm = keep.tile([P, 2], F32, name="warm")
+        nc.gpsimd.memset(warm[:, 0:1], 0.0)
+        nc.scalar.activation(warm[:, 1:2], warm[:, 0:1], SIGMOID)
         offs_t = load_list("offs_t", offs)
+        k1_t = load_list("k1_t", k1)
         w_view = w1.rearrange("(p j) c -> p j c", j=PACK)
         w_raw = [keep.tile([P, PACK, b - a], F32, name="w_raw%d" % a) for a, b in W_PARTS]
         nc.sync.dma_start(w_raw[0][:], w_view[:, :, W_PARTS[0][0] : W_PARTS[0][1]])
-        k1_t = load_list("k1_t", k1)
         for q in range(4):
             nc.sync.dma_start(x_sc[32 * q : 32 * q + 4, :].bitcast(I32), x_scales[0][4 * q : 4 * q + 4, :].bitcast(I32))
         nc.sync.dma_start(d_sc[0:P:8, :].bitcast(I32), d_scales[0].bitcast(I32))
@@ -65,10 +68,10 @@ def tile_picked_densecmptrack_none_p_kernel(
         nc.sync.dma_start(x_w[:].bitcast(I32), x_words[0].rearrange("p n t -> p (n t)").bitcast(I32))
         n2_t = load_list("n2_t", n2)
         n1_t = load_list("n1_t", n1)
-        d_w = keep.tile([P, G], U32, name="d_w")
-        nc.sync.dma_start(d_w[:].bitcast(I32), d_words[0].rearrange("p n t -> p (n t)").bitcast(I32))
         gs_t = keep.tile([P, PACK], F32, name="gs_t")
         nc.sync.dma_start(gs_t[:], gs.rearrange("(p t) o -> p (t o)", t=PACK))
+        d_w = keep.tile([P, G], U32, name="d_w")
+        nc.sync.dma_start(d_w[:].bitcast(I32), d_words[0].rearrange("p n t -> p (n t)").bitcast(I32))
         n3_t = load_list("n3_t", n3)
         n4_t = load_list("n4_t", n4)
 
@@ -87,14 +90,12 @@ def tile_picked_densecmptrack_none_p_kernel(
         nc.vector.tensor_copy(dg_sc[:], d_sc[:].indirect(k1_t[:]))
         xg_w = keep.tile([P, S], U32, name="xg_w", align_bytes=64)
         y_ps = [psum.tile([P, S], F32, name="y_ps%d" % t) for t in range(PACK)]
-        y_sb = [keep.tile([P, 2 * S if t < 2 else S], F32, name="y_sb%d" % t) for t in range(PACK)]
-        for t in range(2):
-            nc.vector.memset(y_sb[t][:, S : 2 * S], 0.0)
+        y_sb = [keep.tile([P, S], F32, name="y_sb%d" % t) for t in range(PACK)]
         for a, b in ((0, 256), (256, 512)):
             nc.vector.tensor_copy(xg_w[:, a:b], x_w[:].indirect(entries(offs_t, a, b)))
         for t in range(PACK):
             m = slice(t * P, (t + 1) * P)
-            for a, b in ((0, 256), (256, 512)):
+            for a, b in ((0, 256), (256, 512)) if t == 0 else ((0, S),):
                 nc.tensor.matmul_mx(
                     out=y_ps[t][:, a:b], lhsT=w_q[:, m].bitcast(FP8X4), lhsT_scale=w_sc[:, m],
                     rhs=xg_w[:, a:b].bitcast(FP8X4), rhs_scale=xg_sc[:, a:b], start=True, stop=True,
@@ -110,45 +111,40 @@ def tile_picked_densecmptrack_none_p_kernel(
         for r in range(1, 4):
             nc.sync.dma_start(dm_sc[r:P:32, :].bitcast(I32), dd_sc[8 * r : P : 32, :].bitcast(I32))
 
-        dg_w = keep.tile([P, H], U32, name="dg_w", align_bytes=64)
-        dd_w = keep.tile([P, H], U32, name="dd_w", align_bytes=64)
-
-        def dictionary_words():
-            nc.vector.tensor_copy(dg_w[:], d_w[:].indirect(k1_t[:]))
-            nc.vector.tensor_copy(
-                dd_w[:].bitcast(I32).rearrange("p (t m) -> p m t", t=PACK),
-                dg_w[:].bitcast(I32).rearrange("p (m t) -> p m t", t=PACK),
-            )
-
         h_ps = [psum.tile([P, S], F32, name="h_ps%d" % t) for t in range(PACK)]
-        h_sb = [keep.tile([P, 2 * S], F32, name="h_sb%d" % t) for t in range(PACK)]
-        for t in range(PACK):
-            (nc.gpsimd if t < 2 else nc.vector).memset(h_sb[t][:, S : 2 * S], 0.0)
-        z_q = keep.tile([P, S], U32, name="z_q", align_bytes=64)
-        z_sc = keep.tile([P, S], U8, name="z_sc", align_bytes=64)
-        units = [(0, 0, 512), (1, 0, 512), (2, 0, 256), (3, 0, 256), (2, 256, 512), (3, 256, 384), (3, 384, 512)]
+        h_sb = [keep.tile([P, S], F32, name="h_sb%d" % t) for t in range(PACK)]
+        z_all = keep.tile([P, PACK, S], BF16, name="z_all")
+        units = [(0, 0, 256), (0, 256, 512), (1, 0, 256), (2, 0, 256), (3, 0, 256), (1, 256, 512),
+                 (2, 256, 512), (3, 256, 384), (3, 384, 512)]
+        on_pool = range(6)
         second = {}
         gates = {}
+        y_gs = {}
 
-        def fetch_second(u):
+        def fetch(u):
             t, a, b = units[u]
-            second[u] = ring.tile([P, b - a], F32, name="second")
+            second[u] = keep.tile([P, b - a], F32, name="second%d" % u, align_bytes=64)
             nc.vector.tensor_copy(second[u][:], y_sb[t][:].indirect(entries(n2_t, a, b)))
 
         def make_gate(u):
             t, a, b = units[u]
-            diff = ring.tile([P, b - a], F32, name="diff")
+            diff = keep.tile([P, b - a], F32, name="diff%d" % u)
             nc.vector.tensor_tensor(diff[:], y_sb[t][:].indirect(entries(n1_t, a, b)), second[u][:], SUB)
-            gates[u] = ring.tile([P, b - a], F32, name="gate", bufs=3)
+            if u in on_pool:
+                y_gs[u] = keep.tile([P, b - a], F32, name="y_gs%d" % u)
+                nc.scalar.activation(y_gs[u][:], y_ps[t][:, a:b], COPY, scale=gs_t[:, t : t + 1])
+            gates[u] = keep.tile([P, b - a], F32, name="gate%d" % u)
             nc.scalar.activation(gates[u][:], diff[:], SIGMOID)
 
         def make_z(u):
             t, a, b = units[u]
-            nc.vector.scalar_tensor_tensor(
-                z_all[:, t, a:b], y_ps[t][:, a:b], gs_t[:, t : t + 1], gates[u][:], MULT, MULT
-            )
+            if u in on_pool:
+                nc.gpsimd.tensor_tensor(z_all[:, t, a:b], y_gs[u][:], gates[u][:], MULT)
+            else:
+                nc.vector.scalar_tensor_tensor(
+                    z_all[:, t, a:b], y_ps[t][:, a:b], gs_t[:, t : t + 1], gates[u][:], MULT, MULT
+                )
 
-        z_all = keep.tile([P, PACK, S], BF16, name="z_all")
         z_bf = {}
 
         def interleave(ci):
@@ -161,48 +157,73 @@ def tile_picked_densecmptrack_none_p_kernel(
             else:
                 nc.scalar.copy(z_dst, z_src)
 
+        z_q = {}
+        z_sc = keep.tile([P, S], U8, name="z_sc", align_bytes=64)
+
         def quantize_z(ci):
             a, b = Z_CHUNKS[ci]
-            nc.vector.quantize_mx(out=z_q[:, a:b].bitcast(FP8X4), scales=z_sc[:, a:b], in_=z_bf[ci][:])
+            half = a // 256
+            nc.vector.quantize_mx(
+                out=z_q[half][:, a - 256 * half : b - 256 * half].bitcast(FP8X4), scales=z_sc[:, a:b], in_=z_bf[ci][:]
+            )
 
         def second_product(t, a, b):
             m = slice(t * P, (t + 1) * P)
+            half = a // 256
             nc.tensor.matmul_mx(
                 out=h_ps[t][:, a:b], lhsT=dd_w[:, m].bitcast(FP8X4), lhsT_scale=dm_sc[:, m],
-                rhs=z_q[:, a:b].bitcast(FP8X4), rhs_scale=z_sc[:, a:b], start=True, stop=True,
+                rhs=z_q[half][:, a - 256 * half : b - 256 * half].bitcast(FP8X4), rhs_scale=z_sc[:, a:b],
+                start=True, stop=True,
             )
 
         def leave_bank(t, a, b):
             nc.scalar.activation(h_sb[t][:, a:b], h_ps[t][:, a:b], COPY, scale=0.0625)
 
-        fetch_second(0)
-        fetch_second(1)
+        def fetch_words(a, b):
+            nc.vector.tensor_copy(dg_w[:, a:b], d_w[:].indirect(entries(k1_t, a, b)))
+
+        fetch(0)
+        fetch(1)
         make_gate(0)
-        fetch_second(2)
         make_gate(1)
         make_z(0)
-        fetch_second(3)
-        make_gate(2)
         make_z(1)
-        fetch_second(4)
+        dg_w = keep.tile([P, H], U32, name="dg_w", tag="second1", align_bytes=64)
+        fetch(2)
+        fetch(3)
+        fetch_words(0, 256)
+        make_gate(2)
         make_gate(3)
         make_z(2)
-        dictionary_words()
         make_z(3)
-        interleave(0)
-        fetch_second(5)
+        fetch(4)
+        fetch(5)
+        fetch_words(256, 512)
+        dd_w = keep.tile([P, H], U32, name="dd_w", align_bytes=64)
+        nc.vector.tensor_copy(
+            dd_w[:].bitcast(I32).rearrange("p (t m) -> p m t", t=PACK),
+            dg_w[:].bitcast(I32).rearrange("p (m t) -> p m t", t=PACK),
+        )
         make_gate(4)
-        fetch_second(6)
         make_gate(5)
-        quantize_z(0)
-        for t in range(PACK):
-            second_product(t, 0, 256)
-        leave_bank(0, 0, 256)
-        make_gate(6)
         make_z(4)
         make_z(5)
-        interleave(1)
+        interleave(0)
+        fetch(6)
+        fetch(7)
+        fetch(8)
+        make_gate(6)
+        make_gate(7)
+        make_gate(8)
+        z_q[0] = keep.tile([P, 256], U32, name="z_q0", align_bytes=64)
+        z_q[1] = keep.tile([P, 256], U32, name="z_q1", align_bytes=64)
+        quantize_z(0)
         make_z(6)
+        second_product(0, 0, 256)
+        leave_bank(0, 0, 256)
+        make_z(7)
+        interleave(1)
+        make_z(8)
         interleave(2)
         quantize_z(1)
         quantize_z(2)
@@ -210,6 +231,7 @@ def tile_picked_densecmptrack_none_p_kernel(
         second_product(0, 384, 512)
         leave_bank(0, 256, 512)
         for t in range(1, PACK):
+            second_product(t, 0, 256)
             second_product(t, 256, 512)
 
         out_view = out.rearrange("(p t) j -> t p j", t=PACK)
@@ -218,8 +240,8 @@ def tile_picked_densecmptrack_none_p_kernel(
         step = [keep.tile([P, S], F32, name="step%d" % t) for t in range(PACK)]
         part = [keep.tile([P, S], F32, name="part%d" % t) for t in range(PACK)]
 
-        def weigh(t):
-            nc.scalar.activation(mix[t][:], h_sb[t][:].indirect(n3_t[:]), SIGMOID)
+        def weigh(t, a, b):
+            nc.scalar.activation(mix[t][:, a:b], h_sb[t][:].indirect(entries(n3_t, a, b)), SIGMOID)
 
         def pick(t, a, b):
             nc.vector.tensor_copy(picked[t][:, a:b], h_sb[t][:].indirect(entries(n4_t, a, b)))
@@ -238,35 +260,21 @@ def tile_picked_densecmptrack_none_p_kernel(
                 nc.vector.scalar_tensor_tensor(res[:], h_ps[t][:, a:b], 0.0625, part[t][:, a:b], MULT, ADD)
             nc.sync.dma_start(out_view[t][:, a:b], res[:])
 
-        leave_bank(1, 0, 256)
-        leave_bank(1, 256, 512)
-        weigh(0)
-        leave_bank(2, 0, 256)
-        leave_bank(2, 256, 512)
-        weigh(1)
-        leave_bank(3, 0, 256)
-        leave_bank(3, 256, 512)
-        weigh(2)
-        weigh(3)
-        pick(0, 0, 256)
-        pick(0, 256, 512)
-        differ(0, 0, 256)
-        scale(0, 0, 256)
-        differ(0, 256, 512)
-        scale(0, 256, 512)
-        finish(0, 0, S)
-        pick(1, 0, S)
-        pick(2, 0, S)
-        differ(1, 0, S)
-        scale(1, 0, S)
-        differ(2, 0, S)
-        scale(2, 0, S)
-        pick(3, 0, S)
+        halves = ((0, 256), (256, 512))
+        for t in range(PACK):
+            if t + 1 < PACK:
+                leave_bank(t + 1, 0, S)
+            for a, b in halves:
+                weigh(t, a, b)
+            for a, b in halves:
+                pick(t, a, b)
+            for a, b in halves:
+                differ(t, a, b)
+            for a, b in halves if t in (0, PACK - 1) else ((0, S),):
+                scale(t, a, b)
+            if t == 0:
+                finish(0, 0, S)
         finish(1, 0, S)
-        differ(3, 0, 256)
-        scale(3, 0, 256)
-        differ(3, 256, 512)
-        scale(3, 256, 512)
         finish(2, 0, S)
-        finish(3, 0, 256)
-        finish(3, 256, 512)
+        for a, b in halves:
+            finish(3, a, b)

@@ -20,14 +20,18 @@ COPY = mybir.ActivationFunctionType.Copy
 
 P = 128
 PACK = 4
-W_PARTS = ((0, 256), (256, 512))
-Z_CHUNKS = ((0, 256), (256, 384), (384, 512))
-OUT_CHUNKS = (
-    ((0, 128), (128, 256), (256, 512)),
-    ((0, 512),),
-    ((0, 512),),
-    ((0, 256), (256, 384), (384, 512)),
-)
+LIST_ROWS = 16
+LINE = 8
+H_SCALE = 0.0625
+HALF = S // 2
+HALVES = ((0, HALF), (HALF, S))
+WHOLE = ((0, S),)
+
+Z_CHUNKS = ((0, HALF), (HALF, 3 * S // 4), (3 * S // 4, S))
+Z_PIECES = ((0, 0, S), (1, 0, S), (2, 0, HALF), (3, 0, HALF), (2, HALF, S), (3,) + Z_CHUNKS[1], (3,) + Z_CHUNKS[2])
+GPSIMD_PIECES = 2
+DIFF_SLOTS = ("diff0", "diff1", "y_gs1", "gate1", "second2", "second3", "second4")
+STORES = 6
 
 
 def tile_picked_densecmptrack_none_p_kernel(
@@ -36,34 +40,31 @@ def tile_picked_densecmptrack_none_p_kernel(
     nc = tc.nc
     with ExitStack() as ctx:
         keep = ctx.enter_context(tc.tile_pool(name="keep", bufs=1))
-        ring = ctx.enter_context(tc.tile_pool(name="ring", bufs=2))
+        results = ctx.enter_context(tc.tile_pool(name="results", bufs=STORES))
         psum = ctx.enter_context(tc.psum_pool(name="psum", bufs=1))
 
         def load_list(name, src):
-            lst = keep.tile([P, S // 16], U16, name=name)
+            lst = keep.tile([P, S // LIST_ROWS], U16, name=name)
             nc.sync.dma_start(lst[:], src)
             return lst
 
         def entries(lst, a, b):
-            return lst[:, a // 16 : b // 16]
+            return lst[:, a // LIST_ROWS : b // LIST_ROWS]
 
         x_sc = keep.tile([P, T], U8, name="x_sc")
         d_sc = keep.tile([P, G], U8, name="d_sc")
         nc.gpsimd.memset(x_sc[:].bitcast(I32), 0)
         nc.vector.memset(d_sc[:].bitcast(I32), 0)
 
-        warm = keep.tile([P, 2], F32, name="warm")
-        nc.gpsimd.memset(warm[:, 0:1], 0.0)
-        nc.scalar.activation(warm[:, 1:2], warm[:, 0:1], SIGMOID)
         offs_t = load_list("offs_t", offs)
         k1_t = load_list("k1_t", k1)
         w_view = w1.rearrange("(p j) c -> p j c", j=PACK)
-        w_raw = [keep.tile([P, PACK, b - a], F32, name="w_raw%d" % a) for a, b in W_PARTS]
-        nc.sync.dma_start(w_raw[0][:], w_view[:, :, W_PARTS[0][0] : W_PARTS[0][1]])
+        w_raw = [keep.tile([P, PACK, b - a], F32, name="w_raw%d" % a) for a, b in HALVES]
+        nc.sync.dma_start(w_raw[0][:], w_view[:, :, 0:HALF])
         for q in range(4):
             nc.sync.dma_start(x_sc[32 * q : 32 * q + 4, :].bitcast(I32), x_scales[0][4 * q : 4 * q + 4, :].bitcast(I32))
         nc.sync.dma_start(d_sc[0:P:8, :].bitcast(I32), d_scales[0].bitcast(I32))
-        nc.sync.dma_start(w_raw[1][:], w_view[:, :, W_PARTS[1][0] : W_PARTS[1][1]])
+        nc.sync.dma_start(w_raw[1][:], w_view[:, :, HALF:H])
         x_w = keep.tile([P, T], U32, name="x_w", tag="x_w", align_bytes=64)
         nc.sync.dma_start(x_w[:].bitcast(I32), x_words[0].rearrange("p n t -> p (n t)").bitcast(I32))
         n2_t = load_list("n2_t", n2)
@@ -80,22 +81,25 @@ def tile_picked_densecmptrack_none_p_kernel(
 
         w_bf = keep.tile([P, PACK * H], BF16, name="w_bf", align_bytes=64)
         w_dst = w_bf[:].rearrange("p (t m j) -> p m j t", t=PACK, j=PACK)
-        nc.scalar.copy(w_dst[:, 0:64], w_raw[0][:].rearrange("p j (m t) -> p m j t", t=PACK))
-        nc.scalar.copy(w_dst[:, 64:128], w_raw[1][:].rearrange("p j (m t) -> p m j t", t=PACK))
+        for half, (a, b) in enumerate(HALVES):
+            nc.scalar.copy(w_dst[:, a // PACK : b // PACK], w_raw[half][:].rearrange("p j (m t) -> p m j t", t=PACK))
         w_q = keep.tile([P, H], U32, name="w_q", align_bytes=64)
         w_sc = keep.tile([P, H], U8, name="w_sc", align_bytes=64)
         nc.vector.quantize_mx(out=w_q[:].bitcast(FP8X4), scales=w_sc[:], in_=w_bf[:])
 
         dg_sc = keep.tile([P, H], U8, name="dg_sc", align_bytes=64)
         nc.vector.tensor_copy(dg_sc[:], d_sc[:].indirect(k1_t[:]))
+
         xg_w = keep.tile([P, S], U32, name="xg_w", align_bytes=64)
         y_ps = [psum.tile([P, S], F32, name="y_ps%d" % t) for t in range(PACK)]
-        y_sb = [keep.tile([P, S], F32, name="y_sb%d" % t) for t in range(PACK)]
-        for a, b in ((0, 256), (256, 512)):
+        y_sb = [keep.tile([P, 2 * S if t < GPSIMD_PIECES else S], F32, name="y_sb%d" % t) for t in range(PACK)]
+        for t in range(GPSIMD_PIECES):
+            nc.vector.memset(y_sb[t][:, S : 2 * S], 0.0)
+        for a, b in HALVES:
             nc.vector.tensor_copy(xg_w[:, a:b], x_w[:].indirect(entries(offs_t, a, b)))
         for t in range(PACK):
             m = slice(t * P, (t + 1) * P)
-            for a, b in ((0, 256), (256, 512)) if t == 0 else ((0, S),):
+            for a, b in HALVES if t == 0 else WHOLE:
                 nc.tensor.matmul_mx(
                     out=y_ps[t][:, a:b], lhsT=w_q[:, m].bitcast(FP8X4), lhsT_scale=w_sc[:, m],
                     rhs=xg_w[:, a:b].bitcast(FP8X4), rhs_scale=xg_sc[:, a:b], start=True, stop=True,
@@ -113,36 +117,32 @@ def tile_picked_densecmptrack_none_p_kernel(
 
         h_ps = [psum.tile([P, S], F32, name="h_ps%d" % t) for t in range(PACK)]
         h_sb = [keep.tile([P, S], F32, name="h_sb%d" % t) for t in range(PACK)]
-        z_all = keep.tile([P, PACK, S], BF16, name="z_all")
-        units = [(0, 0, 256), (0, 256, 512), (1, 0, 256), (2, 0, 256), (3, 0, 256), (1, 256, 512),
-                 (2, 256, 512), (3, 256, 384), (3, 384, 512)]
-        on_pool = range(6)
         second = {}
         gates = {}
         y_gs = {}
 
-        def fetch(u):
-            t, a, b = units[u]
+        def fetch_second(u):
+            t, a, b = Z_PIECES[u]
             second[u] = keep.tile([P, b - a], F32, name="second%d" % u, align_bytes=64)
             nc.vector.tensor_copy(second[u][:], y_sb[t][:].indirect(entries(n2_t, a, b)))
 
         def make_gate(u):
-            t, a, b = units[u]
-            diff = keep.tile([P, b - a], F32, name="diff%d" % u)
+            t, a, b = Z_PIECES[u]
+            diff = keep.tile([P, b - a], F32, name="diff%d" % u, tag=DIFF_SLOTS[u], align_bytes=64)
             nc.vector.tensor_tensor(diff[:], y_sb[t][:].indirect(entries(n1_t, a, b)), second[u][:], SUB)
-            if u in on_pool:
-                y_gs[u] = keep.tile([P, b - a], F32, name="y_gs%d" % u)
+            if u < GPSIMD_PIECES:
+                y_gs[u] = keep.tile([P, b - a], F32, name="y_gs%d" % u, align_bytes=64)
                 nc.scalar.activation(y_gs[u][:], y_ps[t][:, a:b], COPY, scale=gs_t[:, t : t + 1])
-            gates[u] = keep.tile([P, b - a], F32, name="gate%d" % u)
+            gates[u] = keep.tile([P, b - a], F32, name="gate%d" % u, align_bytes=64)
             nc.scalar.activation(gates[u][:], diff[:], SIGMOID)
 
         def make_z(u):
-            t, a, b = units[u]
-            if u in on_pool:
-                nc.gpsimd.tensor_tensor(z_all[:, t, a:b], y_gs[u][:], gates[u][:], MULT)
+            t, a, b = Z_PIECES[u]
+            if u < GPSIMD_PIECES:
+                nc.gpsimd.tensor_tensor(z_rows[:, t, a:b], y_gs[u][:], gates[u][:], MULT)
             else:
                 nc.vector.scalar_tensor_tensor(
-                    z_all[:, t, a:b], y_ps[t][:, a:b], gs_t[:, t : t + 1], gates[u][:], MULT, MULT
+                    z_rows[:, t, a:b], y_ps[t][:, a:b], gs_t[:, t : t + 1], gates[u][:], MULT, MULT
                 )
 
         z_bf = {}
@@ -150,131 +150,118 @@ def tile_picked_densecmptrack_none_p_kernel(
         def interleave(ci):
             a, b = Z_CHUNKS[ci]
             z_bf[ci] = keep.tile([P, PACK * (b - a)], BF16, name="z_bf%d" % ci, align_bytes=64)
-            z_dst = z_bf[ci][:].rearrange("p (c i t) -> p c t i", i=8, t=PACK)
-            z_src = z_all[:, :, a:b].rearrange("p t (c i) -> p c t i", i=8)
+            z_dst = z_bf[ci][:].rearrange("p (c i t) -> p c t i", i=LINE, t=PACK)
+            z_src = z_rows[:, :, a:b].rearrange("p t (c i) -> p c t i", i=LINE)
             if ci == len(Z_CHUNKS) - 1:
                 nc.vector.tensor_copy(z_dst, z_src)
             else:
                 nc.scalar.copy(z_dst, z_src)
 
-        z_q = {}
         z_sc = keep.tile([P, S], U8, name="z_sc", align_bytes=64)
+
+        def z_words(a, b):
+            start = a // HALF * HALF
+            return z_q[a // HALF][:, a - start : b - start].bitcast(FP8X4)
 
         def quantize_z(ci):
             a, b = Z_CHUNKS[ci]
-            half = a // 256
-            nc.vector.quantize_mx(
-                out=z_q[half][:, a - 256 * half : b - 256 * half].bitcast(FP8X4), scales=z_sc[:, a:b], in_=z_bf[ci][:]
-            )
+            nc.vector.quantize_mx(out=z_words(a, b), scales=z_sc[:, a:b], in_=z_bf[ci][:])
 
         def second_product(t, a, b):
             m = slice(t * P, (t + 1) * P)
-            half = a // 256
             nc.tensor.matmul_mx(
                 out=h_ps[t][:, a:b], lhsT=dd_w[:, m].bitcast(FP8X4), lhsT_scale=dm_sc[:, m],
-                rhs=z_q[half][:, a - 256 * half : b - 256 * half].bitcast(FP8X4), rhs_scale=z_sc[:, a:b],
-                start=True, stop=True,
+                rhs=z_words(a, b), rhs_scale=z_sc[:, a:b], start=True, stop=True,
             )
 
-        def leave_bank(t, a, b):
-            nc.scalar.activation(h_sb[t][:, a:b], h_ps[t][:, a:b], COPY, scale=0.0625)
+        def leave_bank(t):
+            nc.scalar.activation(h_sb[t][:], h_ps[t][:], COPY, scale=H_SCALE)
 
-        def fetch_words(a, b):
-            nc.vector.tensor_copy(dg_w[:, a:b], d_w[:].indirect(entries(k1_t, a, b)))
-
-        fetch(0)
-        fetch(1)
+        fetch_second(0)
+        fetch_second(1)
         make_gate(0)
         make_gate(1)
+        z_rows = keep.tile([P, PACK, S], BF16, name="z_rows", tag="second1", align_bytes=64)
         make_z(0)
         make_z(1)
-        dg_w = keep.tile([P, H], U32, name="dg_w", tag="second1", align_bytes=64)
-        fetch(2)
-        fetch(3)
-        fetch_words(0, 256)
+        for u in range(GPSIMD_PIECES, len(Z_PIECES)):
+            fetch_second(u)
+        dg_w = keep.tile([P, H], U32, name="dg_w", tag="diff1", align_bytes=64)
+        nc.vector.tensor_copy(dg_w[:], d_w[:].indirect(k1_t[:]))
         make_gate(2)
         make_gate(3)
+        make_gate(4)
         make_z(2)
         make_z(3)
-        fetch(4)
-        fetch(5)
-        fetch_words(256, 512)
-        dd_w = keep.tile([P, H], U32, name="dd_w", align_bytes=64)
+        make_gate(5)
+        make_gate(6)
+        interleave(0)
+        dd_w = keep.tile([P, H], U32, name="dd_w", tag="second5", align_bytes=64)
         nc.vector.tensor_copy(
             dd_w[:].bitcast(I32).rearrange("p (t m) -> p m t", t=PACK),
             dg_w[:].bitcast(I32).rearrange("p (m t) -> p m t", t=PACK),
         )
-        make_gate(4)
-        make_gate(5)
         make_z(4)
         make_z(5)
-        interleave(0)
-        fetch(6)
-        fetch(7)
-        fetch(8)
-        make_gate(6)
-        make_gate(7)
-        make_gate(8)
-        z_q[0] = keep.tile([P, 256], U32, name="z_q0", align_bytes=64)
-        z_q[1] = keep.tile([P, 256], U32, name="z_q1", align_bytes=64)
-        quantize_z(0)
-        make_z(6)
-        second_product(0, 0, 256)
-        leave_bank(0, 0, 256)
-        make_z(7)
         interleave(1)
-        make_z(8)
+        make_z(6)
+        z_q = [keep.tile([P, HALF], U32, name="z_q%d" % half, align_bytes=64) for half in range(2)]
+        quantize_z(0)
+        second_product(0, *Z_CHUNKS[0])
         interleave(2)
         quantize_z(1)
         quantize_z(2)
-        second_product(0, 256, 384)
-        second_product(0, 384, 512)
-        leave_bank(0, 256, 512)
+        second_product(0, *Z_CHUNKS[1])
+        second_product(0, *Z_CHUNKS[2])
+        leave_bank(0)
         for t in range(1, PACK):
-            second_product(t, 0, 256)
-            second_product(t, 256, 512)
+            for a, b in HALVES:
+                second_product(t, a, b)
 
         out_view = out.rearrange("(p t) j -> t p j", t=PACK)
         mix = [keep.tile([P, S], F32, name="mix%d" % t) for t in range(PACK)]
-        picked = [keep.tile([P, S], F32, name="picked%d" % t) for t in range(PACK)]
-        step = [keep.tile([P, S], F32, name="step%d" % t) for t in range(PACK)]
-        part = [keep.tile([P, S], F32, name="part%d" % t) for t in range(PACK)]
+        picked = {}
+        pull = [keep.tile([P, S], F32, name="pull%d" % t) for t in range(PACK)]
+        part = {}
 
         def weigh(t, a, b):
             nc.scalar.activation(mix[t][:, a:b], h_sb[t][:].indirect(entries(n3_t, a, b)), SIGMOID)
 
         def pick(t, a, b):
-            nc.vector.tensor_copy(picked[t][:, a:b], h_sb[t][:].indirect(entries(n4_t, a, b)))
+            picked[t, a] = keep.tile([P, b - a], F32, name="picked%d" % a)
+            nc.vector.tensor_copy(picked[t, a][:], h_sb[t][:].indirect(entries(n4_t, a, b)))
 
         def differ(t, a, b):
-            nc.vector.scalar_tensor_tensor(step[t][:, a:b], h_ps[t][:, a:b], -0.0625, picked[t][:, a:b], MULT, ADD)
+            nc.vector.scalar_tensor_tensor(pull[t][:, a:b], h_ps[t][:, a:b], -H_SCALE, picked[t, a][:], MULT, ADD)
 
         def scale(t, a, b):
-            nc.gpsimd.tensor_tensor(part[t][:, a:b], step[t][:, a:b], mix[t][:, a:b], MULT)
+            if a == 0:
+                part[t] = keep.tile([P, S], F32, name="part%d" % t)
+            nc.gpsimd.tensor_tensor(part[t][:, a:b], pull[t][:, a:b], mix[t][:, a:b], MULT)
 
         def finish(t, a, b):
-            res = ring.tile([P, b - a], F32, name="res", bufs=5)
+            res = results.tile([P, b - a], F32, name="res")
             if t == 0:
                 nc.gpsimd.tensor_tensor(res[:], part[t][:, a:b], h_sb[t][:, a:b], ADD)
             else:
-                nc.vector.scalar_tensor_tensor(res[:], h_ps[t][:, a:b], 0.0625, part[t][:, a:b], MULT, ADD)
+                nc.vector.scalar_tensor_tensor(res[:], h_ps[t][:, a:b], H_SCALE, part[t][:, a:b], MULT, ADD)
             nc.sync.dma_start(out_view[t][:, a:b], res[:])
 
-        halves = ((0, 256), (256, 512))
+        last = PACK - 1
         for t in range(PACK):
-            if t + 1 < PACK:
-                leave_bank(t + 1, 0, S)
-            for a, b in halves:
+            if t < last:
+                leave_bank(t + 1)
+            for a, b in HALVES:
                 weigh(t, a, b)
-            for a, b in halves:
+            for a, b in HALVES:
                 pick(t, a, b)
-            for a, b in halves:
+            for a, b in HALVES:
                 differ(t, a, b)
-            for a, b in halves if t in (0, PACK - 1) else ((0, S),):
+            for a, b in HALVES if t in (0, last) else WHOLE:
                 scale(t, a, b)
             if t == 0:
-                finish(0, 0, S)
-        finish(1, 0, S)
-        finish(2, 0, S)
-        for a, b in halves:
-            finish(3, a, b)
+                for a, b in HALVES:
+                    finish(t, a, b)
+        for t in range(1, PACK):
+            for a, b in HALVES if t == last else WHOLE:
+                finish(t, a, b)

from contextlib import ExitStack

import concourse.mybir as mybir

K, T, S, H, G = 512, 2048, 512, 512, 2048
FLOPS = 2 * K * H * S + 2 * H * H * S

F32 = mybir.dt.float32
BF16 = mybir.dt.bfloat16
I32 = mybir.dt.int32
U32 = mybir.dt.uint32
U16 = mybir.dt.uint16
U8 = mybir.dt.uint8
FP8X4 = mybir.dt.float8_e4m3fn_x4
MULT = mybir.AluOpType.mult
ADD = mybir.AluOpType.add
SUB = mybir.AluOpType.subtract
SIGMOID = mybir.ActivationFunctionType.Sigmoid
COPY = mybir.ActivationFunctionType.Copy

P = 128
PACK = 4
LIST_ROWS = 16
LINE = 8
H_SCALE = 0.0625
HALF = S // 2
HALVES = ((0, HALF), (HALF, S))
WHOLE = ((0, S),)

Z_CHUNKS = ((0, HALF), (HALF, 3 * S // 4), (3 * S // 4, S))
Z_PIECES = ((0, 0, S), (1, 0, S), (2, 0, HALF), (3, 0, HALF), (2, HALF, S), (3,) + Z_CHUNKS[1], (3,) + Z_CHUNKS[2])
GPSIMD_PIECES = 2
DIFF_SLOTS = ("diff0", "diff1", "y_gs1", "gate1", "second2", "second3", "second4")
STORES = 6


def tile_picked_densecmptrack_none_p_kernel(
    tc, x_words, x_scales, w1, gs, d_words, d_scales, offs, n1, n2, k1, n3, n4, out
):
    nc = tc.nc
    with ExitStack() as ctx:
        keep = ctx.enter_context(tc.tile_pool(name="keep", bufs=1))
        results = ctx.enter_context(tc.tile_pool(name="results", bufs=STORES))
        psum = ctx.enter_context(tc.psum_pool(name="psum", bufs=1))

        def load_list(name, src):
            lst = keep.tile([P, S // LIST_ROWS], U16, name=name)
            nc.sync.dma_start(lst[:], src)
            return lst

        def entries(lst, a, b):
            return lst[:, a // LIST_ROWS : b // LIST_ROWS]

        x_sc = keep.tile([P, T], U8, name="x_sc")
        d_sc = keep.tile([P, G], U8, name="d_sc")
        nc.gpsimd.memset(x_sc[:].bitcast(I32), 0)
        nc.vector.memset(d_sc[:].bitcast(I32), 0)

        offs_t = load_list("offs_t", offs)
        k1_t = load_list("k1_t", k1)
        w_view = w1.rearrange("(p j) c -> p j c", j=PACK)
        w_raw = [keep.tile([P, PACK, b - a], F32, name="w_raw%d" % a) for a, b in HALVES]
        nc.sync.dma_start(w_raw[0][:], w_view[:, :, 0:HALF])
        for q in range(4):
            nc.sync.dma_start(x_sc[32 * q : 32 * q + 4, :].bitcast(I32), x_scales[0][4 * q : 4 * q + 4, :].bitcast(I32))
        nc.sync.dma_start(d_sc[0:P:8, :].bitcast(I32), d_scales[0].bitcast(I32))
        nc.sync.dma_start(w_raw[1][:], w_view[:, :, HALF:H])
        x_w = keep.tile([P, T], U32, name="x_w", tag="x_w", align_bytes=64)
        nc.sync.dma_start(x_w[:].bitcast(I32), x_words[0].rearrange("p n t -> p (n t)").bitcast(I32))
        n2_t = load_list("n2_t", n2)
        n1_t = load_list("n1_t", n1)
        gs_t = keep.tile([P, PACK], F32, name="gs_t")
        nc.sync.dma_start(gs_t[:], gs.rearrange("(p t) o -> p (t o)", t=PACK))
        d_w = keep.tile([P, G], U32, name="d_w")
        nc.sync.dma_start(d_w[:].bitcast(I32), d_words[0].rearrange("p n t -> p (n t)").bitcast(I32))
        n3_t = load_list("n3_t", n3)
        n4_t = load_list("n4_t", n4)

        xg_sc = keep.tile([P, S], U8, name="xg_sc", align_bytes=64)
        nc.vector.tensor_copy(xg_sc[:], x_sc[:].indirect(offs_t[:]))

        w_bf = keep.tile([P, PACK * H], BF16, name="w_bf", align_bytes=64)
        w_dst = w_bf[:].rearrange("p (t m j) -> p m j t", t=PACK, j=PACK)
        for half, (a, b) in enumerate(HALVES):
            nc.scalar.copy(w_dst[:, a // PACK : b // PACK], w_raw[half][:].rearrange("p j (m t) -> p m j t", t=PACK))
        w_q = keep.tile([P, H], U32, name="w_q", align_bytes=64)
        w_sc = keep.tile([P, H], U8, name="w_sc", align_bytes=64)
        nc.vector.quantize_mx(out=w_q[:].bitcast(FP8X4), scales=w_sc[:], in_=w_bf[:])

        dg_sc = keep.tile([P, H], U8, name="dg_sc", align_bytes=64)
        nc.vector.tensor_copy(dg_sc[:], d_sc[:].indirect(k1_t[:]))

        xg_w = keep.tile([P, S], U32, name="xg_w", align_bytes=64)
        y_ps = [psum.tile([P, S], F32, name="y_ps%d" % t) for t in range(PACK)]
        y_sb = [keep.tile([P, 2 * S if t < GPSIMD_PIECES else S], F32, name="y_sb%d" % t) for t in range(PACK)]
        for t in range(GPSIMD_PIECES):
            nc.vector.memset(y_sb[t][:, S : 2 * S], 0.0)
        for a, b in HALVES:
            nc.vector.tensor_copy(xg_w[:, a:b], x_w[:].indirect(entries(offs_t, a, b)))
        for t in range(PACK):
            m = slice(t * P, (t + 1) * P)
            for a, b in HALVES if t == 0 else WHOLE:
                nc.tensor.matmul_mx(
                    out=y_ps[t][:, a:b], lhsT=w_q[:, m].bitcast(FP8X4), lhsT_scale=w_sc[:, m],
                    rhs=xg_w[:, a:b].bitcast(FP8X4), rhs_scale=xg_sc[:, a:b], start=True, stop=True,
                )
                nc.scalar.copy(y_sb[t][:, a:b], y_ps[t][:, a:b])

        dd_sc = keep.tile([P, H], U8, name="dd_sc", tag="x_w", align_bytes=64)
        nc.vector.tensor_copy(
            dd_sc[:].rearrange("p (t m) -> p m t", t=PACK), dg_sc[:].rearrange("p (m t) -> p m t", t=PACK)
        )
        dm_sc = keep.tile([P, H], U8, name="dm_sc", align_bytes=64)
        nc.vector.tensor_copy(dm_sc[:].bitcast(I32), dd_sc[:].bitcast(I32))
        for r in range(1, 4):
            nc.sync.dma_start(dm_sc[r:P:32, :].bitcast(I32), dd_sc[8 * r : P : 32, :].bitcast(I32))

        h_ps = [psum.tile([P, S], F32, name="h_ps%d" % t) for t in range(PACK)]
        h_sb = [keep.tile([P, S], F32, name="h_sb%d" % t) for t in range(PACK)]
        second = {}
        gates = {}
        y_gs = {}

        def fetch_second(u):
            t, a, b = Z_PIECES[u]
            second[u] = keep.tile([P, b - a], F32, name="second%d" % u, align_bytes=64)
            nc.vector.tensor_copy(second[u][:], y_sb[t][:].indirect(entries(n2_t, a, b)))

        def make_gate(u):
            t, a, b = Z_PIECES[u]
            diff = keep.tile([P, b - a], F32, name="diff%d" % u, tag=DIFF_SLOTS[u], align_bytes=64)
            nc.vector.tensor_tensor(diff[:], y_sb[t][:].indirect(entries(n1_t, a, b)), second[u][:], SUB)
            if u < GPSIMD_PIECES:
                y_gs[u] = keep.tile([P, b - a], F32, name="y_gs%d" % u, align_bytes=64)
                nc.scalar.activation(y_gs[u][:], y_ps[t][:, a:b], COPY, scale=gs_t[:, t : t + 1])
            gates[u] = keep.tile([P, b - a], F32, name="gate%d" % u, align_bytes=64)
            nc.scalar.activation(gates[u][:], diff[:], SIGMOID)

        def make_z(u):
            t, a, b = Z_PIECES[u]
            if u < GPSIMD_PIECES:
                nc.gpsimd.tensor_tensor(z_rows[:, t, a:b], y_gs[u][:], gates[u][:], MULT)
            else:
                nc.vector.scalar_tensor_tensor(
                    z_rows[:, t, a:b], y_ps[t][:, a:b], gs_t[:, t : t + 1], gates[u][:], MULT, MULT
                )

        z_bf = {}

        def interleave(ci):
            a, b = Z_CHUNKS[ci]
            z_bf[ci] = keep.tile([P, PACK * (b - a)], BF16, name="z_bf%d" % ci, align_bytes=64)
            z_dst = z_bf[ci][:].rearrange("p (c i t) -> p c t i", i=LINE, t=PACK)
            z_src = z_rows[:, :, a:b].rearrange("p t (c i) -> p c t i", i=LINE)
            if ci == len(Z_CHUNKS) - 1:
                nc.vector.tensor_copy(z_dst, z_src)
            else:
                nc.scalar.copy(z_dst, z_src)

        z_sc = keep.tile([P, S], U8, name="z_sc", align_bytes=64)

        def z_words(a, b):
            start = a // HALF * HALF
            return z_q[a // HALF][:, a - start : b - start].bitcast(FP8X4)

        def quantize_z(ci):
            a, b = Z_CHUNKS[ci]
            nc.vector.quantize_mx(out=z_words(a, b), scales=z_sc[:, a:b], in_=z_bf[ci][:])

        def second_product(t, a, b):
            m = slice(t * P, (t + 1) * P)
            nc.tensor.matmul_mx(
                out=h_ps[t][:, a:b], lhsT=dd_w[:, m].bitcast(FP8X4), lhsT_scale=dm_sc[:, m],
                rhs=z_words(a, b), rhs_scale=z_sc[:, a:b], start=True, stop=True,
            )

        def leave_bank(t):
            nc.scalar.activation(h_sb[t][:], h_ps[t][:], COPY, scale=H_SCALE)

        fetch_second(0)
        fetch_second(1)
        make_gate(0)
        make_gate(1)
        z_rows = keep.tile([P, PACK, S], BF16, name="z_rows", tag="second1", align_bytes=64)
        make_z(0)
        make_z(1)
        for u in range(GPSIMD_PIECES, len(Z_PIECES)):
            fetch_second(u)
        dg_w = keep.tile([P, H], U32, name="dg_w", tag="diff1", align_bytes=64)
        nc.vector.tensor_copy(dg_w[:], d_w[:].indirect(k1_t[:]))
        make_gate(2)
        make_gate(3)
        make_gate(4)
        make_z(2)
        make_z(3)
        make_gate(5)
        make_gate(6)
        interleave(0)
        dd_w = keep.tile([P, H], U32, name="dd_w", tag="second5", align_bytes=64)
        nc.vector.tensor_copy(
            dd_w[:].bitcast(I32).rearrange("p (t m) -> p m t", t=PACK),
            dg_w[:].bitcast(I32).rearrange("p (m t) -> p m t", t=PACK),
        )
        make_z(4)
        make_z(5)
        interleave(1)
        make_z(6)
        z_q = [keep.tile([P, HALF], U32, name="z_q%d" % half, align_bytes=64) for half in range(2)]
        quantize_z(0)
        second_product(0, *Z_CHUNKS[0])
        interleave(2)
        quantize_z(1)
        quantize_z(2)
        second_product(0, *Z_CHUNKS[1])
        second_product(0, *Z_CHUNKS[2])
        leave_bank(0)
        for t in range(1, PACK):
            for a, b in HALVES:
                second_product(t, a, b)

        out_view = out.rearrange("(p t) j -> t p j", t=PACK)
        mix = [keep.tile([P, S], F32, name="mix%d" % t) for t in range(PACK)]
        picked = {}
        pull = [keep.tile([P, S], F32, name="pull%d" % t) for t in range(PACK)]
        part = {}

        def weigh(t, a, b):
            nc.scalar.activation(mix[t][:, a:b], h_sb[t][:].indirect(entries(n3_t, a, b)), SIGMOID)

        def pick(t, a, b):
            picked[t, a] = keep.tile([P, b - a], F32, name="picked%d" % a)
            nc.vector.tensor_copy(picked[t, a][:], h_sb[t][:].indirect(entries(n4_t, a, b)))

        def differ(t, a, b):
            nc.vector.scalar_tensor_tensor(pull[t][:, a:b], h_ps[t][:, a:b], -H_SCALE, picked[t, a][:], MULT, ADD)

        def scale(t, a, b):
            if a == 0:
                part[t] = keep.tile([P, S], F32, name="part%d" % t)
            nc.gpsimd.tensor_tensor(part[t][:, a:b], pull[t][:, a:b], mix[t][:, a:b], MULT)

        def finish(t, a, b):
            res = results.tile([P, b - a], F32, name="res")
            if t == 0:
                nc.gpsimd.tensor_tensor(res[:], part[t][:, a:b], h_sb[t][:, a:b], ADD)
            else:
                nc.vector.scalar_tensor_tensor(res[:], h_ps[t][:, a:b], H_SCALE, part[t][:, a:b], MULT, ADD)
            nc.sync.dma_start(out_view[t][:, a:b], res[:])

        last = PACK - 1
        for t in range(PACK):
            if t < last:
                leave_bank(t + 1)
            for a, b in HALVES:
                weigh(t, a, b)
            for a, b in HALVES:
                pick(t, a, b)
            for a, b in HALVES:
                differ(t, a, b)
            for a, b in HALVES if t in (0, last) else WHOLE:
                scale(t, a, b)
            if t == 0:
                for a, b in HALVES:
                    finish(t, a, b)
        for t in range(1, PACK):
            for a, b in HALVES if t == last else WHOLE:
                finish(t, a, b)
